import numpy as np, ml_dtypes
CORES = [1,9,17,25,33,41,49,57,65,73,81,89,97,105,113,121]
N = 16
COUNTS = [[2,3,1,2,3,1,2,12,1,2,3,1,2,3,1,2],[1,2,3,1,2,3,1,8,3,1,2,3,1,2,3,1],[3,1,2,3,1,2,3,4,2,3,1,2,3,1,2,3],[2,3,1,2,3,1,2,12,1,2,3,1,2,3,1,2],[1,2,3,1,2,3,1,8,3,1,2,3,1,2,3,1],[3,1,2,3,1,2,3,4,2,3,1,2,3,1,2,3],[2,3,1,2,3,1,2,12,1,2,3,1,2,3,1,2],[1,2,3,1,2,3,1,8,3,1,2,3,1,2,3,1],[3,1,2,3,1,2,3,4,2,3,1,2,3,1,2,3],[2,3,1,2,3,1,2,12,1,2,3,1,2,3,1,2],[1,2,3,1,2,3,1,8,3,1,2,3,1,2,3,1],[3,1,2,3,1,2,3,4,2,3,1,2,3,1,2,3],[2,3,1,2,3,1,2,12,1,2,3,1,2,3,1,2],[1,2,3,1,2,3,1,8,3,1,2,3,1,2,3,1],[3,1,2,3,1,2,3,4,2,3,1,2,3,1,2,3],[2,3,1,2,3,1,2,12,1,2,3,1,2,3,1,2]]
XW, YW = 41, 132
def setup_inputs(rng):
    return {"x": rng.standard_normal((N, 128, XW), dtype=np.float32).astype(ml_dtypes.bfloat16)}
def reference(x):
    y = np.full((N, 128, YW), np.nan, x.dtype)
    fill = [0] * N
    for s in range(N):
        o = 0
        for d in range(N):
            c = COUNTS[s][d]
            y[d][:, fill[d]:fill[d] + c] = x[s][:, o:o + c]
            o += c; fill[d] += c
    return {"y": y}

@@ -1,0 +1,113 @@
+import concourse.bass as bass
+
+SCRATCH = {
+    "xs": ("sbuf", [128, 41], "bfloat16"),
+    "land": ("sbuf", [128, 132], "bfloat16"),
+}
+SEMAPHORES = ["loaded", "own", "got", "arrived", "sent", "stored"]
+
+RANK_K = 1
+CROSS_CORES = (6, 2, 3, 7)
+SAME_HELPERS = (4, 5, 0)
+
+
+def bits(m):
+    return bin(m).count("1")
+
+
+def units_of(row, ds):
+    byw = {}
+    for d in ds:
+        byw.setdefault(row[d], []).append(d)
+    pairs, singles = [], []
+    for w in sorted(byw, reverse=True):
+        l = byw[w]
+        for i in range(0, len(l) - 1, 2):
+            pairs.append([(l[i], 0x0F), (l[i + 1], 0xF0)])
+        if len(l) % 2:
+            singles.append([(l[-1], 0xFF)])
+    return pairs, singles
+
+
+def plan(s, C):
+    n = len(C)
+    row = C[s]
+
+    def width(unit):
+        return sum(row[d] for call in unit for d, m in call)
+
+    pairs, singles = units_of(row, [d for d in range(n) if (d ^ s) & 1])
+    units = [[p] for p in pairs] + [singles[i:i + 2] for i in range(0, len(singles), 2)]
+    units.sort(key=width, reverse=True)
+    calls = dict(zip(CROSS_CORES, units))
+    pairs, singles = units_of(row, [d for d in range(n) if not (d ^ s) & 1 and d != s])
+    if singles:
+        calls[RANK_K] = singles[:2]
+        rest = [[p] for p in pairs] + [[c] for c in singles[2:]]
+    else:
+        calls[RANK_K] = [pairs[0]]
+        rest = [[p] for p in pairs[1:]]
+    rest.sort(key=width, reverse=True)
+    calls.update(zip(SAME_HELPERS, rest))
+    order = sorted(CROSS_CORES, key=lambda k: -len(calls[k])) + [k for k in SAME_HELPERS if k in calls]
+    return calls, order
+
+
+def rank_program(g, core, T, topo):
+    C = T.tables["COUNTS"]
+    cores = T.cores
+    n = len(cores)
+    chip = topo.chip(core)
+    k = core % 8
+    s = [r for r in range(n) if topo.chip(cores[r]) == chip][0]
+    calls, order = plan(s, C)
+    if k not in calls:
+        return
+    sent = 0
+
+    if k == RANK_K:
+        own_x = sum(C[s][:s])
+        own_y = sum(C[t][s] for t in range(s))
+        w = C[s][s]
+        g.dma_start(T.xs[:], T.x[:]).then_inc(T.sem.loaded, 16)
+        g.dma_start(T.land[:, own_y:own_y + w], T.x[:, own_x:own_x + w]).then_inc(T.sem.own, 16)
+        g.wait_ge(T.sem.loaded, 16)
+        ids = []
+        for h in order:
+            rid, pid, se = topo.addr(chip * 8 + h)
+            ids.append(bass.DstId(rid=rid, pnc=pid))
+        g.remote_dma_fused(
+            [bass.RemoteDMATransfer(dst_ids=ids, dma_engine_mask=0xFFFF, remote_sem=T.sem.got,
+                                    srcs=[T.xs[:]], dsts=[T.xs[:] for h in order])],
+            local_sem=T.sem.sent)
+        sent += 16
+    else:
+        g.wait_ge(T.sem.got, 16)
+
+    for call in calls[k]:
+        trs = []
+        for d, m in call:
+            rid, pid, se = topo.addr(cores[d])
+            xo = sum(C[s][:d])
+            yo = sum(C[t][d] for t in range(s))
+            w = C[s][d]
+            trs.append(bass.RemoteDMATransfer(dst_ids=[bass.DstId(rid=rid, pnc=pid)], dma_engine_mask=m,
+                                              remote_sem=T.sem.arrived,
+                                              src=T.xs[:, xo:xo + w], dst=T.land[:, yo:yo + w]))
+            sent += bits(m)
+        g.remote_dma_fused(trs, local_sem=T.sem.sent)
+
+    if k == RANK_K:
+        due = 0
+        for t in range(n):
+            if t != s:
+                for cl in plan(t, C)[0].values():
+                    due += sum(bits(m) for call in cl for d, m in call if d == s)
+        tot = sum(C[t][s] for t in range(n))
+        g.wait_ge(T.sem.own, 16)
+        g.wait_ge(T.sem.arrived, due)
+        g.dma_start(T.y[:, 0:tot], T.land[:, 0:tot]).then_inc(T.sem.stored, 16)
+        g.wait_ge(T.sem.sent, sent)
+        g.wait_ge(T.sem.stored, 16)
+    else:
+        g.wait_ge(T.sem.sent, sent)

@@ -7,50 +7,60 @@ SCRATCH = {
 SEMAPHORES = ["loaded", "own", "got", "arrived", "sent", "stored"]
 
 RANK_K = 1
-CROSS_CORES = (6, 2, 3, 7)
-SAME_HELPERS = (4, 5, 0)
+PAIR_CORES = (2, 3, 7)
+ODD_K = 6
+SAME_K = 4
+HELPERS = PAIR_CORES + (ODD_K, SAME_K)
 
 
 def bits(m):
     return bin(m).count("1")
 
 
-def units_of(row, ds):
+def pair(a, b):
+    return [(a, 0x0F), (b, 0xF0)]
+
+
+def lone(a):
+    return [(a, 0xFF)]
+
+
+def by_width(row, ds):
     byw = {}
     for d in ds:
         byw.setdefault(row[d], []).append(d)
-    pairs, singles = [], []
-    for w in sorted(byw, reverse=True):
-        l = byw[w]
-        for i in range(0, len(l) - 1, 2):
-            pairs.append([(l[i], 0x0F), (l[i + 1], 0xF0)])
-        if len(l) % 2:
-            singles.append([(l[-1], 0xFF)])
-    return pairs, singles
+    return byw
+
+
+def take_pair(same):
+    w = max(v for v in same if len(same[v]) >= 2)
+    return pair(same[w].pop(0), same[w].pop(0))
 
 
 def plan(s, C):
     n = len(C)
     row = C[s]
-
-    def width(unit):
-        return sum(row[d] for call in unit for d, m in call)
-
-    pairs, singles = units_of(row, [d for d in range(n) if (d ^ s) & 1])
-    units = [[p] for p in pairs] + [singles[i:i + 2] for i in range(0, len(singles), 2)]
-    units.sort(key=width, reverse=True)
-    calls = dict(zip(CROSS_CORES, units))
-    pairs, singles = units_of(row, [d for d in range(n) if not (d ^ s) & 1 and d != s])
-    if singles:
-        calls[RANK_K] = singles[:2]
-        rest = [[p] for p in pairs] + [[c] for c in singles[2:]]
+    cross = by_width(row, [d for d in range(n) if (d ^ s) & 1])
+    same = by_width(row, [d for d in range(n) if not (d ^ s) & 1 and d != s])
+    pairs, odd = [], []
+    for w in sorted(cross, reverse=True):
+        l = cross[w]
+        for i in range(0, len(l) - 1, 2):
+            pairs.append(pair(l[i], l[i + 1]))
+        if len(l) % 2:
+            odd.append(l[-1])
+    top = max(same)
+    if len(same[top]) == 1:
+        mine = [lone(same[top].pop())]
+        w = max([v for v in same if len(same[v]) % 2] or [v for v in same if same[v]])
+        mine.append(lone(same[w].pop()))
     else:
-        calls[RANK_K] = [pairs[0]]
-        rest = [[p] for p in pairs[1:]]
-    rest.sort(key=width, reverse=True)
-    calls.update(zip(SAME_HELPERS, rest))
-    order = sorted(CROSS_CORES, key=lambda k: -len(calls[k])) + [k for k in SAME_HELPERS if k in calls]
-    return calls, order
+        mine = [take_pair(same)]
+    calls = {RANK_K: mine, SAME_K: [take_pair(same)], ODD_K: [lone(d) for d in odd]}
+    rest = [d for v in sorted(same, reverse=True) for d in same[v]]
+    for k, p, d in zip(PAIR_CORES, pairs, rest):
+        calls[k] = [p, lone(d)]
+    return calls
 
 
 def rank_program(g, core, T, topo):
@@ -60,7 +70,7 @@ def rank_program(g, core, T, topo):
     chip = topo.chip(core)
     k = core % 8
     s = [r for r in range(n) if topo.chip(cores[r]) == chip][0]
-    calls, order = plan(s, C)
+    calls = plan(s, C)
     if k not in calls:
         return
     sent = 0
@@ -68,17 +78,17 @@ def rank_program(g, core, T, topo):
     if k == RANK_K:
         own_x = sum(C[s][:s])
         own_y = sum(C[t][s] for t in range(s))
-        w = C[s][s]
+        own_w = C[s][s]
         g.dma_start(T.xs[:], T.x[:]).then_inc(T.sem.loaded, 16)
-        g.dma_start(T.land[:, own_y:own_y + w], T.x[:, own_x:own_x + w]).then_inc(T.sem.own, 16)
+        g.dma_start(T.land[:, own_y:own_y + own_w], T.x[:, own_x:own_x + own_w]).then_inc(T.sem.own, 16)
         g.wait_ge(T.sem.loaded, 16)
         ids = []
-        for h in order:
+        for h in HELPERS:
             rid, pid, se = topo.addr(chip * 8 + h)
             ids.append(bass.DstId(rid=rid, pnc=pid))
         g.remote_dma_fused(
             [bass.RemoteDMATransfer(dst_ids=ids, dma_engine_mask=0xFFFF, remote_sem=T.sem.got,
-                                    srcs=[T.xs[:]], dsts=[T.xs[:] for h in order])],
+                                    srcs=[T.xs[:]], dsts=[T.xs[:] for h in HELPERS])],
             local_sem=T.sem.sent)
         sent += 16
     else:
@@ -101,7 +111,7 @@ def rank_program(g, core, T, topo):
         due = 0
         for t in range(n):
             if t != s:
-                for cl in plan(t, C)[0].values():
+                for cl in plan(t, C).values():
                     due += sum(bits(m) for call in cl for d, m in call if d == s)
         tot = sum(C[t][s] for t in range(n))
         g.wait_ge(T.sem.own, 16)

import concourse.bass as bass

SCRATCH = {
    "xs": ("sbuf", [128, 41], "bfloat16"),
    "land": ("sbuf", [128, 132], "bfloat16"),
}
SEMAPHORES = ["loaded", "own", "got", "arrived", "sent", "stored"]

RANK_K = 1
PAIR_CORES = (2, 3, 7)
ODD_K = 6
SAME_K = 4
HELPERS = PAIR_CORES + (ODD_K, SAME_K)


def bits(m):
    return bin(m).count("1")


def pair(a, b):
    return [(a, 0x0F), (b, 0xF0)]


def lone(a):
    return [(a, 0xFF)]


def by_width(row, ds):
    byw = {}
    for d in ds:
        byw.setdefault(row[d], []).append(d)
    return byw


def take_pair(same):
    w = max(v for v in same if len(same[v]) >= 2)
    return pair(same[w].pop(0), same[w].pop(0))


def plan(s, C):
    n = len(C)
    row = C[s]
    cross = by_width(row, [d for d in range(n) if (d ^ s) & 1])
    same = by_width(row, [d for d in range(n) if not (d ^ s) & 1 and d != s])
    pairs, odd = [], []
    for w in sorted(cross, reverse=True):
        l = cross[w]
        for i in range(0, len(l) - 1, 2):
            pairs.append(pair(l[i], l[i + 1]))
        if len(l) % 2:
            odd.append(l[-1])
    top = max(same)
    if len(same[top]) == 1:
        mine = [lone(same[top].pop())]
        w = max([v for v in same if len(same[v]) % 2] or [v for v in same if same[v]])
        mine.append(lone(same[w].pop()))
    else:
        mine = [take_pair(same)]
    calls = {RANK_K: mine, SAME_K: [take_pair(same)], ODD_K: [lone(d) for d in odd]}
    rest = [d for v in sorted(same, reverse=True) for d in same[v]]
    for k, p, d in zip(PAIR_CORES, pairs, rest):
        calls[k] = [p, lone(d)]
    return calls


def rank_program(g, core, T, topo):
    C = T.tables["COUNTS"]
    cores = T.cores
    n = len(cores)
    chip = topo.chip(core)
    k = core % 8
    s = [r for r in range(n) if topo.chip(cores[r]) == chip][0]
    calls = plan(s, C)
    if k not in calls:
        return
    sent = 0

    if k == RANK_K:
        own_x = sum(C[s][:s])
        own_y = sum(C[t][s] for t in range(s))
        own_w = C[s][s]
        g.dma_start(T.xs[:], T.x[:]).then_inc(T.sem.loaded, 16)
        g.dma_start(T.land[:, own_y:own_y + own_w], T.x[:, own_x:own_x + own_w]).then_inc(T.sem.own, 16)
        g.wait_ge(T.sem.loaded, 16)
        ids = []
        for h in HELPERS:
            rid, pid, se = topo.addr(chip * 8 + h)
            ids.append(bass.DstId(rid=rid, pnc=pid))
        g.remote_dma_fused(
            [bass.RemoteDMATransfer(dst_ids=ids, dma_engine_mask=0xFFFF, remote_sem=T.sem.got,
                                    srcs=[T.xs[:]], dsts=[T.xs[:] for h in HELPERS])],
            local_sem=T.sem.sent)
        sent += 16
    else:
        g.wait_ge(T.sem.got, 16)

    for call in calls[k]:
        trs = []
        for d, m in call:
            rid, pid, se = topo.addr(cores[d])
            xo = sum(C[s][:d])
            yo = sum(C[t][d] for t in range(s))
            w = C[s][d]
            trs.append(bass.RemoteDMATransfer(dst_ids=[bass.DstId(rid=rid, pnc=pid)], dma_engine_mask=m,
                                              remote_sem=T.sem.arrived,
                                              src=T.xs[:, xo:xo + w], dst=T.land[:, yo:yo + w]))
            sent += bits(m)
        g.remote_dma_fused(trs, local_sem=T.sem.sent)

    if k == RANK_K:
        due = 0
        for t in range(n):
            if t != s:
                for cl in plan(t, C).values():
                    due += sum(bits(m) for call in cl for d, m in call if d == s)
        tot = sum(C[t][s] for t in range(n))
        g.wait_ge(T.sem.own, 16)
        g.wait_ge(T.sem.arrived, due)
        g.dma_start(T.y[:, 0:tot], T.land[:, 0:tot]).then_inc(T.sem.stored, 16)
        g.wait_ge(T.sem.sent, sent)
        g.wait_ge(T.sem.stored, 16)
    else:
        g.wait_ge(T.sem.sent, sent)
